import numpy as np, ml_dtypes
CORES = [1,17,65,89,97,113]
N = 6
import mx_ref
NC = 256
BF = ml_dtypes.bfloat16
def cut(t, i, w=512):
    return t[:, w * i:w * i + w]
def term(a, B):
    return np.stack([mx_ref.matmul(mx_ref.quantize(cut(a, i)), B) for i in range(4)], axis=2).reshape(128, -1)
def setup_inputs(rng):
    def f(*shape):
        return mx_ref.flush((rng.standard_normal(shape, dtype=np.float32) * np.exp2(rng.integers(-2, 3, shape[:-1] + (1,)))).astype(BF))
    return {"a": f(N, 128, 4 * 512), "b": f(N, 128, N * 4 * NC)}
def setup_inputs_blocks(rng):
    d = setup_inputs(rng)
    for k in ("a", "b"): d[k] = mx_ref.spread(d[k], rng, 2)
    return d
def setup_inputs_wide(rng):
    d = setup_inputs(rng)
    for k in ("a", "b"): d[k] = mx_ref.flush((d[k].astype(np.float32) * np.exp2(rng.integers(-4, 5, (N, 1, 1))).astype(np.float32)).astype(BF))
    return d
def setup_inputs_lossless(rng):
    a = np.zeros((N, 128, 4 * 128, 4), np.float32)
    for r in range(N):
        k = rng.integers(0, 512, size=4 * 128)
        a[r, k // 4, np.arange(4 * 128), k % 4] = 1.0
    size = np.repeat(2.0 ** rng.integers(-4, 5, size=(1, 1, (N * 4 * NC) // 4)), 4, axis=2)
    b = rng.integers(-1, 2, size=(N, 128, N * 4 * NC)) * size
    return {"a": a.reshape(N, 128, 4 * 512).astype(BF), "b": b.astype(np.float32).astype(BF)}
def reference(a, b):
    y = np.zeros((N, 128, 4 * NC), np.float32)
    for c in range(N):
        y[c] = mx_ref.total([term(a[r], mx_ref.quantize(cut(b[r], c, 4 * NC))) for r in range(N)])
    return {"y": y}

@@ -1,0 +1,217 @@
+from concourse.mybir import dt, AluOpType, ActivationFunctionType
+
+N = 6
+NW = 256
+HW = NW // 2
+CHUNKS = [(1, 0, NW, False), (2, 0, NW, True), (3, 0, NW, False), (4, 0, NW, True),
+          (5, 0, HW, True), (5, HW, HW, False)]
+NQ = len(CHUNKS)
+WINDOW = 4
+NLOAD = 2 + NQ + 1
+
+SCRATCH = {
+    "a_sb": ("sbuf", [128, 2048], "bfloat16"),
+    "b_sb": ("sbuf", [128, N * 4 * NW], "bfloat16"),
+    "aq": ("sbuf", [128, 512], "float8_e4m3fn_x4"),
+    "ap": ("sbuf", [128, 512], "uint8"),
+    "bq": ("sbuf", [128, N * NW], "float8_e4m3fn_x4"),
+    "bp": ("sbuf", [128, N * NW], "uint8"),
+    "sel": ("sbuf", [128, 2048], "bfloat16"),
+    "sq": ("sbuf", [128, 512], "float8_e4m3fn_x4"),
+    "sp": ("sbuf", [128, 512], "uint8"),
+    "h": ("sbuf", [128, (N - 1) * 4 * NW], "bfloat16"),
+    "tq": ("sbuf", [128, (N - 1) * NW], "float8_e4m3fn_x4"),
+    "tp": ("sbuf", [128, (N - 1) * NW], "uint8"),
+    "lq": ("sbuf", [128, (N - 1) * NW], "float8_e4m3fn_x4"),
+    "lp": ("sbuf", [128, (N - 1) * NW], "uint8"),
+    "ps": ("psum", [128, 8 * 512], "float32"),
+    "y_sb": ("sbuf", [128, 4 * NW], "float32"),
+}
+SEMAPHORES = (["ld%d" % j for j in range(NLOAD)]
+              + ["hc%d" % q for q in range(NQ)] + ["hp%d" % q for q in range(NQ)]
+              + ["ar%d" % q for q in range(NQ)]
+              + ["ones", "selok", "qa", "qb", "qs", "qt", "pe", "evv", "evs", "dn", "fv", "fs",
+                 "st0", "st1", "sent"])
+
+
+def _engines(mask):
+    return bin(mask).count("1")
+
+
+def _forwarders(T, topo, R):
+    all_cores = range(topo.CHIPS * topo.CORES_PER_CHIP)
+    ok = [c for c in all_cores
+          if topo.chip(c) == topo.chip(R) and c not in T.cores
+          and all(topo.may_write(c, d) for d in T.cores)]
+    near = [c for c in ok if topo.die(c) == topo.die(R)]
+    far = [c for c in ok if topo.die(c) != topo.die(R)]
+    return near[0], far[0]
+
+
+def _send(g, T, topo, src, dst, out_q, out_p, in_q, in_p, lo, hi, sem_q, sem_p):
+    rid, pid, _ = topo.addr(dst)
+    m = topo.mask(src, dst)
+    g.remote_dma(out_q[:, lo:hi].bitcast(dt.uint8), in_q[:, lo:hi].bitcast(dt.uint8),
+                 sem_q, T.sem.sent, pid, rid, m)
+    return rid, pid, m
+
+
+def _forward_program(g, core, T, topo, r, far):
+    total = 0
+    for q, (k, w0, nw, f) in enumerate(CHUNKS):
+        if f != far:
+            continue
+        dst = T.cores[(r + k) % N]
+        rid, pid, _ = topo.addr(dst)
+        m = topo.mask(core, dst)
+        lo = NW * (k - 1) + w0
+        hi = lo + nw
+        n_in = _engines(topo.mask(T.cores[r], core))
+        g.wait_ge(T.sem["hc%d" % q], n_in)
+        g.remote_dma(T.lq[:, lo:hi].bitcast(dt.uint8), T.tq[:, lo:hi].bitcast(dt.uint8),
+                     T.sem["ar%d" % q], T.sem.sent, pid, rid, m)
+        g.wait_ge(T.sem["hp%d" % q], n_in)
+        g.remote_dma(T.lp[:, lo:hi], T.tp[:, lo:hi], T.sem["ar%d" % q], T.sem.sent, pid, rid, m)
+        total += 2 * _engines(m)
+    g.wait_ge(T.sem.sent, total)
+
+
+def _rank_program(g, core, T, topo, r):
+    sem = T.sem
+    v, s, t, sy = g.vector, g.scalar, g.tensor, g.sync
+    near, far = _forwarders(T, topo, core)
+
+    pieces = [(T.a_sb[:, 0:1024], T.a[:, 0:1024]), (T.a_sb[:, 1024:2048], T.a[:, 1024:2048])]
+    for (k, w0, nw, f) in CHUNKS:
+        c = (r + k) % N
+        pieces.append((T.b_sb[:, 4 * (NW * (k - 1) + w0):4 * (NW * (k - 1) + w0 + nw)],
+                       T.b[:, 4 * (NW * c + w0):4 * (NW * c + w0 + nw)]))
+    own0 = NW * (N - 1)
+    pieces.append((T.b_sb[:, 4 * own0:4 * (own0 + NW)], T.b[:, 4 * NW * r:4 * NW * (r + 1)]))
+    for j, (o, i_) in enumerate(pieces):
+        if j < WINDOW:
+            (sy if j % 2 == 0 else s).dma_start(o, i_).then_inc(sem["ld%d" % j], 16)
+        else:
+            sy.wait_ge(sem["ld%d" % (j - WINDOW)], 16)
+            sy.dma_start(o, i_).then_inc(sem["ld%d" % j], 16)
+
+    v.memset(T.sel[:], 1.0).then_inc(sem.ones, 1)
+    g.wait_ge(sem.ones, 1)
+    g.affine_select(T.sel[:], T.sel[:], [[1, 4], [-1, 512]], AluOpType.is_equal, 0.0, 0, 4).then_inc(sem.selok, 1)
+
+    def bank(set_, i, n):
+        b = 4 * set_ + i
+        return T.ps[:, 512 * b:512 * b + n]
+
+    def words(q):
+        k, w0, nw, f = CHUNKS[q]
+        lo = NW * (k - 1) + w0
+        return lo, lo + nw
+
+    def quant_b(q):
+        lo, hi = words(q) if q < NQ else (own0, own0 + NW)
+        v.wait_ge(sem["ld%d" % (2 + q)], 16)
+        v.quantize_mx(T.bq[:, lo:hi], T.bp[:, lo:hi], T.b_sb[:, 4 * lo:4 * hi]).then_inc(sem.qb, 1)
+
+    for j in range(2):
+        v.wait_ge(sem["ld%d" % j], 16)
+        v.quantize_mx(T.aq[:, 256 * j:256 * j + 256], T.ap[:, 256 * j:256 * j + 256],
+                      T.a_sb[:, 1024 * j:1024 * j + 1024]).then_inc(sem.qa, 1)
+    quant_b(0)
+    v.wait_ge(sem.selok, 1)
+    v.quantize_mx(T.sq[:], T.sp[:], T.sel[:]).then_inc(sem.qs, 1)
+    quant_b(1)
+    for q in range(NQ):
+        lo, hi = words(q)
+        for i in (1, 3):
+            v.wait_ge(sem.pe, 4 * q + i + 1)
+            v.tensor_copy(T.h[:, 4 * lo + i:4 * hi:4], bank(q % 2, i, hi - lo)).then_inc(sem.evv, 1)
+        v.wait_ge(sem.evv, 2 * q + 2)
+        v.wait_ge(sem.evs, 2 * q + 2)
+        v.quantize_mx(T.tq[:, lo:hi], T.tp[:, lo:hi], T.h[:, 4 * lo:4 * hi]).then_inc(sem.qt, 1)
+        if q + 2 <= NQ:
+            quant_b(q + 2)
+    for q in range(NQ):
+        lo, hi = words(q)
+        for i in (0, 2):
+            s.wait_ge(sem.pe, 4 * q + i + 1)
+            s.activation(T.h[:, 4 * lo + i:4 * hi:4], bank(q % 2, i, hi - lo),
+                         ActivationFunctionType.Copy).then_inc(sem.evs, 1)
+
+    def a_tile(i):
+        return T.aq[:, 128 * i:128 * i + 128], T.ap[:, 128 * i:128 * i + 128]
+
+    t.wait_ge(sem.qa, 2)
+    for q in range(NQ):
+        lo, hi = words(q)
+        t.wait_ge(sem.qb, q + 1)
+        for i in range(4):
+            if q >= 2:
+                t.wait_ge(sem.evs if i % 2 == 0 else sem.evv, 2 * (q - 2) + i // 2 + 1)
+            aq, ap = a_tile(i)
+            t.matmul_mx(bank(q % 2, i, hi - lo), aq, ap, T.bq[:, lo:hi], T.bp[:, lo:hi],
+                        True, True).then_inc(sem.pe, 1)
+    t.wait_ge(sem.qb, NQ + 1)
+    for hf in range(2):
+        t.wait_ge(sem.evs, 2 * (NQ - 2 + hf) + 2)
+        t.wait_ge(sem.evv, 2 * (NQ - 2 + hf) + 2)
+        lo = own0 + HW * hf
+        for i in range(4):
+            aq, ap = a_tile(i)
+            t.matmul_mx(bank(hf, i, HW), aq, ap, T.bq[:, lo:lo + HW], T.bp[:, lo:lo + HW], True, False)
+    t.wait_ge(sem.qs, 1)
+    for q in range(NQ):
+        k, w0, nw, f = CHUNKS[q]
+        src_fw = _forwarders(T, topo, T.cores[(r - k) % N])[1 if f else 0]
+        t.wait_ge(sem["ar%d" % q], 2 * _engines(topo.mask(src_fw, core)))
+        last = k == N - 1
+        for w in range(w0, w0 + nw, HW):
+            hf = w // HW
+            lo = NW * (k - 1) + w
+            for i in range(4):
+                mm = t.matmul_mx(bank(hf, i, HW), T.sq[:, 128 * i:128 * i + 128], T.sp[:, 128 * i:128 * i + 128],
+                                 T.lq[:, lo:lo + HW], T.lp[:, lo:lo + HW], False, last)
+                if last:
+                    mm.then_inc(sem.dn, 1)
+
+    for hf in range(2):
+        c0, c1 = 4 * HW * hf, 4 * HW * (hf + 1)
+        for i in (0, 2):
+            s.wait_ge(sem.dn, 4 * hf + i + 1)
+            s.activation(T.y_sb[:, c0 + i:c1:4], bank(hf, i, HW), ActivationFunctionType.Copy).then_inc(sem.fs, 1)
+        for i in (1, 3):
+            v.wait_ge(sem.dn, 4 * hf + i + 1)
+            v.tensor_copy(T.y_sb[:, c0 + i:c1:4], bank(hf, i, HW)).then_inc(sem.fv, 1)
+        sy.wait_ge(sem.fs, 2 * hf + 2)
+        sy.wait_ge(sem.fv, 2 * hf + 2)
+        sy.dma_start(T.y[:, c0:c1], T.y_sb[:, c0:c1]).then_inc(sem["st%d" % hf], 16)
+    sy.wait_ge(sem.st0, 16)
+    sy.wait_ge(sem.st1, 16)
+
+    total = 0
+    for q, (k, w0, nw, f) in enumerate(CHUNKS):
+        lo, hi = words(q)
+        fw = far if f else near
+        rid, pid, _ = topo.addr(fw)
+        m = topo.mask(core, fw)
+        g.wait_ge(sem.qt, q + 1)
+        g.remote_dma(T.tq[:, lo:hi].bitcast(dt.uint8), T.tq[:, lo:hi].bitcast(dt.uint8),
+                     sem["hc%d" % q], sem.sent, pid, rid, m)
+        g.remote_dma(T.tp[:, lo:hi], T.tp[:, lo:hi], sem["hp%d" % q], sem.sent, pid, rid, m)
+        total += 2 * _engines(m)
+    g.wait_ge(sem.sent, total)
+
+
+def rank_program(g, core, T, topo):
+    rank = T.rank_of(core)
+    if rank is not None:
+        _rank_program(g, core, T, topo, rank)
+        return
+    for r, R in enumerate(T.cores):
+        if topo.chip(R) != topo.chip(core):
+            continue
+        near, far = _forwarders(T, topo, R)
+        if core == near:
+            _forward_program(g, core, T, topo, r, False)
+        elif core == far:
+            _forward_program(g, core, T, topo, r, True)

@@ -6,7 +6,7 @@ HW = NW // 2
 CHUNKS = [(1, 0, NW, False), (2, 0, NW, True), (3, 0, NW, False), (4, 0, NW, True),
           (5, 0, HW, True), (5, HW, HW, False)]
 NQ = len(CHUNKS)
-WINDOW = 4
+WINDOW = 5
 NLOAD = 2 + NQ + 1
 
 SCRATCH = {
@@ -16,7 +16,7 @@ SCRATCH = {
     "ap": ("sbuf", [128, 512], "uint8"),
     "bq": ("sbuf", [128, N * NW], "float8_e4m3fn_x4"),
     "bp": ("sbuf", [128, N * NW], "uint8"),
-    "sel": ("sbuf", [128, 2048], "bfloat16"),
+    "sel": ("sbuf", [128, 520], "bfloat16"),
     "sq": ("sbuf", [128, 512], "float8_e4m3fn_x4"),
     "sp": ("sbuf", [128, 512], "uint8"),
     "h": ("sbuf", [128, (N - 1) * 4 * NW], "bfloat16"),
@@ -45,41 +45,35 @@ def _forwarders(T, topo, R):
           and all(topo.may_write(c, d) for d in T.cores)]
     near = [c for c in ok if topo.die(c) == topo.die(R)]
     far = [c for c in ok if topo.die(c) != topo.die(R)]
-    return near[0], far[0]
+    return {(False, False): near[0], (False, True): near[-1],
+            (True, False): far[0], (True, True): far[-1]}
 
 
-def _send(g, T, topo, src, dst, out_q, out_p, in_q, in_p, lo, hi, sem_q, sem_p):
-    rid, pid, _ = topo.addr(dst)
-    m = topo.mask(src, dst)
-    g.remote_dma(out_q[:, lo:hi].bitcast(dt.uint8), in_q[:, lo:hi].bitcast(dt.uint8),
-                 sem_q, T.sem.sent, pid, rid, m)
-    return rid, pid, m
-
-
-def _forward_program(g, core, T, topo, r, far):
+def _forward_program(g, core, T, topo, r, roles):
     total = 0
+    n_in = _engines(topo.mask(T.cores[r], core))
     for q, (k, w0, nw, f) in enumerate(CHUNKS):
-        if f != far:
-            continue
         dst = T.cores[(r + k) % N]
         rid, pid, _ = topo.addr(dst)
         m = topo.mask(core, dst)
         lo = NW * (k - 1) + w0
         hi = lo + nw
-        n_in = _engines(topo.mask(T.cores[r], core))
-        g.wait_ge(T.sem["hc%d" % q], n_in)
-        g.remote_dma(T.lq[:, lo:hi].bitcast(dt.uint8), T.tq[:, lo:hi].bitcast(dt.uint8),
-                     T.sem["ar%d" % q], T.sem.sent, pid, rid, m)
-        g.wait_ge(T.sem["hp%d" % q], n_in)
-        g.remote_dma(T.lp[:, lo:hi], T.tp[:, lo:hi], T.sem["ar%d" % q], T.sem.sent, pid, rid, m)
-        total += 2 * _engines(m)
+        if (f, False) in roles:
+            g.wait_ge(T.sem["hc%d" % q], n_in)
+            g.remote_dma(T.lq[:, lo:hi].bitcast(dt.uint8), T.tq[:, lo:hi].bitcast(dt.uint8),
+                         T.sem["ar%d" % q], T.sem.sent, pid, rid, m)
+            total += _engines(m)
+        if (f, True) in roles:
+            g.wait_ge(T.sem["hp%d" % q], n_in)
+            g.remote_dma(T.lp[:, lo:hi], T.tp[:, lo:hi], T.sem["ar%d" % q], T.sem.sent, pid, rid, m)
+            total += _engines(m)
     g.wait_ge(T.sem.sent, total)
 
 
 def _rank_program(g, core, T, topo, r):
     sem = T.sem
     v, s, t, sy = g.vector, g.scalar, g.tensor, g.sync
-    near, far = _forwarders(T, topo, core)
+    fwd = _forwarders(T, topo, core)
 
     pieces = [(T.a_sb[:, 0:1024], T.a[:, 0:1024]), (T.a_sb[:, 1024:2048], T.a[:, 1024:2048])]
     for (k, w0, nw, f) in CHUNKS:
@@ -97,7 +91,7 @@ def _rank_program(g, core, T, topo, r):
 
     v.memset(T.sel[:], 1.0).then_inc(sem.ones, 1)
     g.wait_ge(sem.ones, 1)
-    g.affine_select(T.sel[:], T.sel[:], [[1, 4], [-1, 512]], AluOpType.is_equal, 0.0, 0, 4).then_inc(sem.selok, 1)
+    g.affine_select(T.sel[:], T.sel[:], [[-1, 520]], AluOpType.is_equal, 0.0, 3, 4).then_inc(sem.selok, 1)
 
     def bank(set_, i, n):
         b = 4 * set_ + i
@@ -113,27 +107,29 @@ def _rank_program(g, core, T, topo, r):
         v.wait_ge(sem["ld%d" % (2 + q)], 16)
         v.quantize_mx(T.bq[:, lo:hi], T.bp[:, lo:hi], T.b_sb[:, 4 * lo:4 * hi]).then_inc(sem.qb, 1)
 
+    v.wait_ge(sem.selok, 1)
+    for i in range(4):
+        v.quantize_mx(T.sq[:, 128 * i:128 * i + 128], T.sp[:, 128 * i:128 * i + 128],
+                      T.sel[:, 3 - i:3 - i + 512]).then_inc(sem.qs, 1)
     for j in range(2):
         v.wait_ge(sem["ld%d" % j], 16)
         v.quantize_mx(T.aq[:, 256 * j:256 * j + 256], T.ap[:, 256 * j:256 * j + 256],
                       T.a_sb[:, 1024 * j:1024 * j + 1024]).then_inc(sem.qa, 1)
     quant_b(0)
-    v.wait_ge(sem.selok, 1)
-    v.quantize_mx(T.sq[:], T.sp[:], T.sel[:]).then_inc(sem.qs, 1)
     quant_b(1)
     for q in range(NQ):
         lo, hi = words(q)
-        for i in (1, 3):
-            v.wait_ge(sem.pe, 4 * q + i + 1)
-            v.tensor_copy(T.h[:, 4 * lo + i:4 * hi:4], bank(q % 2, i, hi - lo)).then_inc(sem.evv, 1)
-        v.wait_ge(sem.evv, 2 * q + 2)
-        v.wait_ge(sem.evs, 2 * q + 2)
+        v.wait_ge(sem.pe, 4 * q + 4)
+        v.tensor_copy(T.h[:, 4 * lo + 3:4 * hi:4], bank(q % 2, 3, hi - lo)).then_inc(sem.evv, 1)
+        v.wait_ge(sem.evv, q + 1)
+        v.wait_ge(sem.evs, 3 * q + 3)
         v.quantize_mx(T.tq[:, lo:hi], T.tp[:, lo:hi], T.h[:, 4 * lo:4 * hi]).then_inc(sem.qt, 1)
-        if q + 2 <= NQ:
+        if q + 2 < NQ:
             quant_b(q + 2)
+    quant_b(NQ)
     for q in range(NQ):
         lo, hi = words(q)
-        for i in (0, 2):
+        for i in range(3):
             s.wait_ge(sem.pe, 4 * q + i + 1)
             s.activation(T.h[:, 4 * lo + i:4 * hi:4], bank(q % 2, i, hi - lo),
                          ActivationFunctionType.Copy).then_inc(sem.evs, 1)
@@ -147,32 +143,36 @@ def _rank_program(g, core, T, topo, r):
         t.wait_ge(sem.qb, q + 1)
         for i in range(4):
             if q >= 2:
-                t.wait_ge(sem.evs if i % 2 == 0 else sem.evv, 2 * (q - 2) + i // 2 + 1)
+                if i < 3:
+                    t.wait_ge(sem.evs, 3 * (q - 2) + i + 1)
+                else:
+                    t.wait_ge(sem.evv, q - 1)
             aq, ap = a_tile(i)
             t.matmul_mx(bank(q % 2, i, hi - lo), aq, ap, T.bq[:, lo:hi], T.bp[:, lo:hi],
                         True, True).then_inc(sem.pe, 1)
-    t.wait_ge(sem.qb, NQ + 1)
-    for hf in range(2):
-        t.wait_ge(sem.evs, 2 * (NQ - 2 + hf) + 2)
-        t.wait_ge(sem.evv, 2 * (NQ - 2 + hf) + 2)
-        lo = own0 + HW * hf
-        for i in range(4):
-            aq, ap = a_tile(i)
-            t.matmul_mx(bank(hf, i, HW), aq, ap, T.bq[:, lo:lo + HW], T.bp[:, lo:lo + HW], True, False)
-    t.wait_ge(sem.qs, 1)
+    t.wait_ge(sem.evs, 3 * NQ)
+    t.wait_ge(sem.evv, NQ)
+    t.wait_ge(sem.qs, 4)
     for q in range(NQ):
         k, w0, nw, f = CHUNKS[q]
-        src_fw = _forwarders(T, topo, T.cores[(r - k) % N])[1 if f else 0]
-        t.wait_ge(sem["ar%d" % q], 2 * _engines(topo.mask(src_fw, core)))
+        src = _forwarders(T, topo, T.cores[(r - k) % N])
+        t.wait_ge(sem["ar%d" % q], _engines(topo.mask(src[(f, False)], core)) + _engines(topo.mask(src[(f, True)], core)))
         last = k == N - 1
         for w in range(w0, w0 + nw, HW):
             hf = w // HW
             lo = NW * (k - 1) + w
             for i in range(4):
                 mm = t.matmul_mx(bank(hf, i, HW), T.sq[:, 128 * i:128 * i + 128], T.sp[:, 128 * i:128 * i + 128],
-                                 T.lq[:, lo:lo + HW], T.lp[:, lo:lo + HW], False, last)
+                                 T.lq[:, lo:lo + HW], T.lp[:, lo:lo + HW], q == 0, last)
                 if last:
                     mm.then_inc(sem.dn, 1)
+        if q == 0:
+            t.wait_ge(sem.qb, NQ + 1)
+            for hf in range(2):
+                lo = own0 + HW * hf
+                for i in range(4):
+                    aq, ap = a_tile(i)
+                    t.matmul_mx(bank(hf, i, HW), aq, ap, T.bq[:, lo:lo + HW], T.bp[:, lo:lo + HW], False, False)
 
     for hf in range(2):
         c0, c1 = 4 * HW * hf, 4 * HW * (hf + 1)
@@ -191,14 +191,16 @@ def _rank_program(g, core, T, topo, r):
     total = 0
     for q, (k, w0, nw, f) in enumerate(CHUNKS):
         lo, hi = words(q)
-        fw = far if f else near
-        rid, pid, _ = topo.addr(fw)
-        m = topo.mask(core, fw)
         g.wait_ge(sem.qt, q + 1)
+        rid, pid, _ = topo.addr(fwd[(f, False)])
+        m = topo.mask(core, fwd[(f, False)])
         g.remote_dma(T.tq[:, lo:hi].bitcast(dt.uint8), T.tq[:, lo:hi].bitcast(dt.uint8),
                      sem["hc%d" % q], sem.sent, pid, rid, m)
+        total += _engines(m)
+        rid, pid, _ = topo.addr(fwd[(f, True)])
+        m = topo.mask(core, fwd[(f, True)])
         g.remote_dma(T.tp[:, lo:hi], T.tp[:, lo:hi], sem["hp%d" % q], sem.sent, pid, rid, m)
-        total += 2 * _engines(m)
+        total += _engines(m)
     g.wait_ge(sem.sent, total)
 
 
@@ -210,8 +212,6 @@ def rank_program(g, core, T, topo):
     for r, R in enumerate(T.cores):
         if topo.chip(R) != topo.chip(core):
             continue
-        near, far = _forwarders(T, topo, R)
-        if core == near:
-            _forward_program(g, core, T, topo, r, False)
-        elif core == far:
-            _forward_program(g, core, T, topo, r, True)
+        roles = [role for role, c in _forwarders(T, topo, R).items() if c == core]
+        if roles:
+            _forward_program(g, core, T, topo, r, roles)

@@ -3,10 +3,11 @@ from concourse.mybir import dt, AluOpType, ActivationFunctionType
 N = 6
 NW = 256
 HW = NW // 2
-CHUNKS = [(1, 0, NW, False), (2, 0, NW, True), (3, 0, NW, False), (4, 0, NW, True),
-          (5, 0, HW, True), (5, HW, HW, False)]
+N0, N1, F0, F1 = (False, 0), (False, 1), (True, 0), (True, 1)
+CHUNKS = [(1, 0, HW, F0, F1), (1, HW, HW, N0, N1), (2, 0, NW, F1, N1), (3, 0, NW, N0, F0),
+          (4, 0, NW, N1, F1), (5, 0, HW, F0, F1), (5, HW, HW, N0, F0)]
 NQ = len(CHUNKS)
-WINDOW = 5
+WINDOW = 6
 NLOAD = 2 + NQ + 1
 
 SCRATCH = {
@@ -45,25 +46,24 @@ def _forwarders(T, topo, R):
           and all(topo.may_write(c, d) for d in T.cores)]
     near = [c for c in ok if topo.die(c) == topo.die(R)]
     far = [c for c in ok if topo.die(c) != topo.die(R)]
-    return {(False, False): near[0], (False, True): near[-1],
-            (True, False): far[0], (True, True): far[-1]}
+    return {N0: near[0], N1: near[-1], F0: far[0], F1: far[-1]}
 
 
 def _forward_program(g, core, T, topo, r, roles):
     total = 0
     n_in = _engines(topo.mask(T.cores[r], core))
-    for q, (k, w0, nw, f) in enumerate(CHUNKS):
+    for q, (k, w0, nw, fc, fp) in enumerate(CHUNKS):
         dst = T.cores[(r + k) % N]
         rid, pid, _ = topo.addr(dst)
         m = topo.mask(core, dst)
         lo = NW * (k - 1) + w0
         hi = lo + nw
-        if (f, False) in roles:
+        if fc in roles:
             g.wait_ge(T.sem["hc%d" % q], n_in)
             g.remote_dma(T.lq[:, lo:hi].bitcast(dt.uint8), T.tq[:, lo:hi].bitcast(dt.uint8),
                          T.sem["ar%d" % q], T.sem.sent, pid, rid, m)
             total += _engines(m)
-        if (f, True) in roles:
+        if fp in roles:
             g.wait_ge(T.sem["hp%d" % q], n_in)
             g.remote_dma(T.lp[:, lo:hi], T.tp[:, lo:hi], T.sem["ar%d" % q], T.sem.sent, pid, rid, m)
             total += _engines(m)
@@ -76,17 +76,19 @@ def _rank_program(g, core, T, topo, r):
     fwd = _forwarders(T, topo, core)
 
     pieces = [(T.a_sb[:, 0:1024], T.a[:, 0:1024]), (T.a_sb[:, 1024:2048], T.a[:, 1024:2048])]
-    for (k, w0, nw, f) in CHUNKS:
+    for (k, w0, nw, fc, fp) in CHUNKS:
         c = (r + k) % N
         pieces.append((T.b_sb[:, 4 * (NW * (k - 1) + w0):4 * (NW * (k - 1) + w0 + nw)],
                        T.b[:, 4 * (NW * c + w0):4 * (NW * c + w0 + nw)]))
     own0 = NW * (N - 1)
     pieces.append((T.b_sb[:, 4 * own0:4 * (own0 + NW)], T.b[:, 4 * NW * r:4 * NW * (r + 1)]))
-    for j, (o, i_) in enumerate(pieces):
-        if j < WINDOW:
-            (sy if j % 2 == 0 else s).dma_start(o, i_).then_inc(sem["ld%d" % j], 16)
+    order = [0, 2, 1] + list(range(3, NLOAD))
+    for n, j in enumerate(order):
+        o, i_ = pieces[j]
+        if n < WINDOW:
+            (sy if n % 2 == 0 else s).dma_start(o, i_).then_inc(sem["ld%d" % j], 16)
         else:
-            sy.wait_ge(sem["ld%d" % (j - WINDOW)], 16)
+            sy.wait_ge(sem["ld%d" % order[n - WINDOW]], 16)
             sy.dma_start(o, i_).then_inc(sem["ld%d" % j], 16)
 
     v.memset(T.sel[:], 1.0).then_inc(sem.ones, 1)
@@ -98,9 +100,14 @@ def _rank_program(g, core, T, topo, r):
         return T.ps[:, 512 * b:512 * b + n]
 
     def words(q):
-        k, w0, nw, f = CHUNKS[q]
+        k, w0, nw = CHUNKS[q][:3]
         lo = NW * (k - 1) + w0
         return lo, lo + nw
+
+    def quant_a(j):
+        v.wait_ge(sem["ld%d" % j], 16)
+        v.quantize_mx(T.aq[:, 256 * j:256 * j + 256], T.ap[:, 256 * j:256 * j + 256],
+                      T.a_sb[:, 1024 * j:1024 * j + 1024]).then_inc(sem.qa, 1)
 
     def quant_b(q):
         lo, hi = words(q) if q < NQ else (own0, own0 + NW)
@@ -111,11 +118,9 @@ def _rank_program(g, core, T, topo, r):
     for i in range(4):
         v.quantize_mx(T.sq[:, 128 * i:128 * i + 128], T.sp[:, 128 * i:128 * i + 128],
                       T.sel[:, 3 - i:3 - i + 512]).then_inc(sem.qs, 1)
-    for j in range(2):
-        v.wait_ge(sem["ld%d" % j], 16)
-        v.quantize_mx(T.aq[:, 256 * j:256 * j + 256], T.ap[:, 256 * j:256 * j + 256],
-                      T.a_sb[:, 1024 * j:1024 * j + 1024]).then_inc(sem.qa, 1)
+    quant_a(0)
     quant_b(0)
+    quant_a(1)
     quant_b(1)
     for q in range(NQ):
         lo, hi = words(q)
@@ -137,11 +142,12 @@ def _rank_program(g, core, T, topo, r):
     def a_tile(i):
         return T.aq[:, 128 * i:128 * i + 128], T.ap[:, 128 * i:128 * i + 128]
 
-    t.wait_ge(sem.qa, 2)
     for q in range(NQ):
         lo, hi = words(q)
         t.wait_ge(sem.qb, q + 1)
         for i in range(4):
+            if q == 0 and i % 2 == 0:
+                t.wait_ge(sem.qa, i // 2 + 1)
             if q >= 2:
                 if i < 3:
                     t.wait_ge(sem.evs, 3 * (q - 2) + i + 1)
@@ -154,19 +160,19 @@ def _rank_program(g, core, T, topo, r):
     t.wait_ge(sem.evv, NQ)
     t.wait_ge(sem.qs, 4)
     for q in range(NQ):
-        k, w0, nw, f = CHUNKS[q]
+        k, w0, nw, fc, fp = CHUNKS[q]
         src = _forwarders(T, topo, T.cores[(r - k) % N])
-        t.wait_ge(sem["ar%d" % q], _engines(topo.mask(src[(f, False)], core)) + _engines(topo.mask(src[(f, True)], core)))
+        t.wait_ge(sem["ar%d" % q], _engines(topo.mask(src[fc], core)) + _engines(topo.mask(src[fp], core)))
         last = k == N - 1
         for w in range(w0, w0 + nw, HW):
             hf = w // HW
             lo = NW * (k - 1) + w
             for i in range(4):
                 mm = t.matmul_mx(bank(hf, i, HW), T.sq[:, 128 * i:128 * i + 128], T.sp[:, 128 * i:128 * i + 128],
-                                 T.lq[:, lo:lo + HW], T.lp[:, lo:lo + HW], q == 0, last)
+                                 T.lq[:, lo:lo + HW], T.lp[:, lo:lo + HW], k == 1, last)
                 if last:
                     mm.then_inc(sem.dn, 1)
-        if q == 0:
+        if k == 1 and CHUNKS[q + 1][0] != 1:
             t.wait_ge(sem.qb, NQ + 1)
             for hf in range(2):
                 lo = own0 + HW * hf
@@ -189,16 +195,16 @@ def _rank_program(g, core, T, topo, r):
     sy.wait_ge(sem.st1, 16)
 
     total = 0
-    for q, (k, w0, nw, f) in enumerate(CHUNKS):
+    for q, (k, w0, nw, fc, fp) in enumerate(CHUNKS):
         lo, hi = words(q)
         g.wait_ge(sem.qt, q + 1)
-        rid, pid, _ = topo.addr(fwd[(f, False)])
-        m = topo.mask(core, fwd[(f, False)])
+        rid, pid, _ = topo.addr(fwd[fc])
+        m = topo.mask(core, fwd[fc])
         g.remote_dma(T.tq[:, lo:hi].bitcast(dt.uint8), T.tq[:, lo:hi].bitcast(dt.uint8),
                      sem["hc%d" % q], sem.sent, pid, rid, m)
         total += _engines(m)
-        rid, pid, _ = topo.addr(fwd[(f, True)])
-        m = topo.mask(core, fwd[(f, True)])
+        rid, pid, _ = topo.addr(fwd[fp])
+        m = topo.mask(core, fwd[fp])
         g.remote_dma(T.tp[:, lo:hi], T.tp[:, lo:hi], sem["hp%d" % q], sem.sent, pid, rid, m)
         total += _engines(m)
     g.wait_ge(sem.sent, total)

from concourse.mybir import dt, AluOpType, ActivationFunctionType

N = 6
NW = 256
HW = NW // 2
N0, N1, F0, F1 = (False, 0), (False, 1), (True, 0), (True, 1)
CHUNKS = [(1, 0, HW, F0, F1), (1, HW, HW, N0, N1), (2, 0, NW, F1, N1), (3, 0, NW, N0, F0),
          (4, 0, NW, N1, F1), (5, 0, HW, F0, F1), (5, HW, HW, N0, F0)]
NQ = len(CHUNKS)
WINDOW = 6
NLOAD = 2 + NQ + 1

SCRATCH = {
    "a_sb": ("sbuf", [128, 2048], "bfloat16"),
    "b_sb": ("sbuf", [128, N * 4 * NW], "bfloat16"),
    "aq": ("sbuf", [128, 512], "float8_e4m3fn_x4"),
    "ap": ("sbuf", [128, 512], "uint8"),
    "bq": ("sbuf", [128, N * NW], "float8_e4m3fn_x4"),
    "bp": ("sbuf", [128, N * NW], "uint8"),
    "sel": ("sbuf", [128, 520], "bfloat16"),
    "sq": ("sbuf", [128, 512], "float8_e4m3fn_x4"),
    "sp": ("sbuf", [128, 512], "uint8"),
    "h": ("sbuf", [128, (N - 1) * 4 * NW], "bfloat16"),
    "tq": ("sbuf", [128, (N - 1) * NW], "float8_e4m3fn_x4"),
    "tp": ("sbuf", [128, (N - 1) * NW], "uint8"),
    "lq": ("sbuf", [128, (N - 1) * NW], "float8_e4m3fn_x4"),
    "lp": ("sbuf", [128, (N - 1) * NW], "uint8"),
    "ps": ("psum", [128, 8 * 512], "float32"),
    "y_sb": ("sbuf", [128, 4 * NW], "float32"),
}
SEMAPHORES = (["ld%d" % j for j in range(NLOAD)]
              + ["hc%d" % q for q in range(NQ)] + ["hp%d" % q for q in range(NQ)]
              + ["ar%d" % q for q in range(NQ)]
              + ["ones", "selok", "qa", "qb", "qs", "qt", "pe", "evv", "evs", "dn", "fv", "fs",
                 "st0", "st1", "sent"])


def _engines(mask):
    return bin(mask).count("1")


def _forwarders(T, topo, R):
    all_cores = range(topo.CHIPS * topo.CORES_PER_CHIP)
    ok = [c for c in all_cores
          if topo.chip(c) == topo.chip(R) and c not in T.cores
          and all(topo.may_write(c, d) for d in T.cores)]
    near = [c for c in ok if topo.die(c) == topo.die(R)]
    far = [c for c in ok if topo.die(c) != topo.die(R)]
    return {N0: near[0], N1: near[-1], F0: far[0], F1: far[-1]}


def _forward_program(g, core, T, topo, r, roles):
    total = 0
    n_in = _engines(topo.mask(T.cores[r], core))
    for q, (k, w0, nw, fc, fp) in enumerate(CHUNKS):
        dst = T.cores[(r + k) % N]
        rid, pid, _ = topo.addr(dst)
        m = topo.mask(core, dst)
        lo = NW * (k - 1) + w0
        hi = lo + nw
        if fc in roles:
            g.wait_ge(T.sem["hc%d" % q], n_in)
            g.remote_dma(T.lq[:, lo:hi].bitcast(dt.uint8), T.tq[:, lo:hi].bitcast(dt.uint8),
                         T.sem["ar%d" % q], T.sem.sent, pid, rid, m)
            total += _engines(m)
        if fp in roles:
            g.wait_ge(T.sem["hp%d" % q], n_in)
            g.remote_dma(T.lp[:, lo:hi], T.tp[:, lo:hi], T.sem["ar%d" % q], T.sem.sent, pid, rid, m)
            total += _engines(m)
    g.wait_ge(T.sem.sent, total)


def _rank_program(g, core, T, topo, r):
    sem = T.sem
    v, s, t, sy = g.vector, g.scalar, g.tensor, g.sync
    fwd = _forwarders(T, topo, core)

    pieces = [(T.a_sb[:, 0:1024], T.a[:, 0:1024]), (T.a_sb[:, 1024:2048], T.a[:, 1024:2048])]
    for (k, w0, nw, fc, fp) in CHUNKS:
        c = (r + k) % N
        pieces.append((T.b_sb[:, 4 * (NW * (k - 1) + w0):4 * (NW * (k - 1) + w0 + nw)],
                       T.b[:, 4 * (NW * c + w0):4 * (NW * c + w0 + nw)]))
    own0 = NW * (N - 1)
    pieces.append((T.b_sb[:, 4 * own0:4 * (own0 + NW)], T.b[:, 4 * NW * r:4 * NW * (r + 1)]))
    order = [0, 2, 1] + list(range(3, NLOAD))
    for n, j in enumerate(order):
        o, i_ = pieces[j]
        if n < WINDOW:
            (sy if n % 2 == 0 else s).dma_start(o, i_).then_inc(sem["ld%d" % j], 16)
        else:
            sy.wait_ge(sem["ld%d" % order[n - WINDOW]], 16)
            sy.dma_start(o, i_).then_inc(sem["ld%d" % j], 16)

    v.memset(T.sel[:], 1.0).then_inc(sem.ones, 1)
    g.wait_ge(sem.ones, 1)
    g.affine_select(T.sel[:], T.sel[:], [[-1, 520]], AluOpType.is_equal, 0.0, 3, 4).then_inc(sem.selok, 1)

    def bank(set_, i, n):
        b = 4 * set_ + i
        return T.ps[:, 512 * b:512 * b + n]

    def words(q):
        k, w0, nw = CHUNKS[q][:3]
        lo = NW * (k - 1) + w0
        return lo, lo + nw

    def quant_a(j):
        v.wait_ge(sem["ld%d" % j], 16)
        v.quantize_mx(T.aq[:, 256 * j:256 * j + 256], T.ap[:, 256 * j:256 * j + 256],
                      T.a_sb[:, 1024 * j:1024 * j + 1024]).then_inc(sem.qa, 1)

    def quant_b(q):
        lo, hi = words(q) if q < NQ else (own0, own0 + NW)
        v.wait_ge(sem["ld%d" % (2 + q)], 16)
        v.quantize_mx(T.bq[:, lo:hi], T.bp[:, lo:hi], T.b_sb[:, 4 * lo:4 * hi]).then_inc(sem.qb, 1)

    v.wait_ge(sem.selok, 1)
    for i in range(4):
        v.quantize_mx(T.sq[:, 128 * i:128 * i + 128], T.sp[:, 128 * i:128 * i + 128],
                      T.sel[:, 3 - i:3 - i + 512]).then_inc(sem.qs, 1)
    quant_a(0)
    quant_b(0)
    quant_a(1)
    quant_b(1)
    for q in range(NQ):
        lo, hi = words(q)
        v.wait_ge(sem.pe, 4 * q + 4)
        v.tensor_copy(T.h[:, 4 * lo + 3:4 * hi:4], bank(q % 2, 3, hi - lo)).then_inc(sem.evv, 1)
        v.wait_ge(sem.evv, q + 1)
        v.wait_ge(sem.evs, 3 * q + 3)
        v.quantize_mx(T.tq[:, lo:hi], T.tp[:, lo:hi], T.h[:, 4 * lo:4 * hi]).then_inc(sem.qt, 1)
        if q + 2 < NQ:
            quant_b(q + 2)
    quant_b(NQ)
    for q in range(NQ):
        lo, hi = words(q)
        for i in range(3):
            s.wait_ge(sem.pe, 4 * q + i + 1)
            s.activation(T.h[:, 4 * lo + i:4 * hi:4], bank(q % 2, i, hi - lo),
                         ActivationFunctionType.Copy).then_inc(sem.evs, 1)

    def a_tile(i):
        return T.aq[:, 128 * i:128 * i + 128], T.ap[:, 128 * i:128 * i + 128]

    for q in range(NQ):
        lo, hi = words(q)
        t.wait_ge(sem.qb, q + 1)
        for i in range(4):
            if q == 0 and i % 2 == 0:
                t.wait_ge(sem.qa, i // 2 + 1)
            if q >= 2:
                if i < 3:
                    t.wait_ge(sem.evs, 3 * (q - 2) + i + 1)
                else:
                    t.wait_ge(sem.evv, q - 1)
            aq, ap = a_tile(i)
            t.matmul_mx(bank(q % 2, i, hi - lo), aq, ap, T.bq[:, lo:hi], T.bp[:, lo:hi],
                        True, True).then_inc(sem.pe, 1)
    t.wait_ge(sem.evs, 3 * NQ)
    t.wait_ge(sem.evv, NQ)
    t.wait_ge(sem.qs, 4)
    for q in range(NQ):
        k, w0, nw, fc, fp = CHUNKS[q]
        src = _forwarders(T, topo, T.cores[(r - k) % N])
        t.wait_ge(sem["ar%d" % q], _engines(topo.mask(src[fc], core)) + _engines(topo.mask(src[fp], core)))
        last = k == N - 1
        for w in range(w0, w0 + nw, HW):
            hf = w // HW
            lo = NW * (k - 1) + w
            for i in range(4):
                mm = t.matmul_mx(bank(hf, i, HW), T.sq[:, 128 * i:128 * i + 128], T.sp[:, 128 * i:128 * i + 128],
                                 T.lq[:, lo:lo + HW], T.lp[:, lo:lo + HW], k == 1, last)
                if last:
                    mm.then_inc(sem.dn, 1)
        if k == 1 and CHUNKS[q + 1][0] != 1:
            t.wait_ge(sem.qb, NQ + 1)
            for hf in range(2):
                lo = own0 + HW * hf
                for i in range(4):
                    aq, ap = a_tile(i)
                    t.matmul_mx(bank(hf, i, HW), aq, ap, T.bq[:, lo:lo + HW], T.bp[:, lo:lo + HW], False, False)

    for hf in range(2):
        c0, c1 = 4 * HW * hf, 4 * HW * (hf + 1)
        for i in (0, 2):
            s.wait_ge(sem.dn, 4 * hf + i + 1)
            s.activation(T.y_sb[:, c0 + i:c1:4], bank(hf, i, HW), ActivationFunctionType.Copy).then_inc(sem.fs, 1)
        for i in (1, 3):
            v.wait_ge(sem.dn, 4 * hf + i + 1)
            v.tensor_copy(T.y_sb[:, c0 + i:c1:4], bank(hf, i, HW)).then_inc(sem.fv, 1)
        sy.wait_ge(sem.fs, 2 * hf + 2)
        sy.wait_ge(sem.fv, 2 * hf + 2)
        sy.dma_start(T.y[:, c0:c1], T.y_sb[:, c0:c1]).then_inc(sem["st%d" % hf], 16)
    sy.wait_ge(sem.st0, 16)
    sy.wait_ge(sem.st1, 16)

    total = 0
    for q, (k, w0, nw, fc, fp) in enumerate(CHUNKS):
        lo, hi = words(q)
        g.wait_ge(sem.qt, q + 1)
        rid, pid, _ = topo.addr(fwd[fc])
        m = topo.mask(core, fwd[fc])
        g.remote_dma(T.tq[:, lo:hi].bitcast(dt.uint8), T.tq[:, lo:hi].bitcast(dt.uint8),
                     sem["hc%d" % q], sem.sent, pid, rid, m)
        total += _engines(m)
        rid, pid, _ = topo.addr(fwd[fp])
        m = topo.mask(core, fwd[fp])
        g.remote_dma(T.tp[:, lo:hi], T.tp[:, lo:hi], sem["hp%d" % q], sem.sent, pid, rid, m)
        total += _engines(m)
    g.wait_ge(sem.sent, total)


def rank_program(g, core, T, topo):
    rank = T.rank_of(core)
    if rank is not None:
        _rank_program(g, core, T, topo, rank)
        return
    for r, R in enumerate(T.cores):
        if topo.chip(R) != topo.chip(core):
            continue
        roles = [role for role, c in _forwarders(T, topo, R).items() if c == core]
        if roles:
            _forward_program(g, core, T, topo, r, roles)
